import numpy as np
import ml_dtypes


def mxq(x, axis, fmt="e4m3"):
    dtype, down = {"e4m3": (ml_dtypes.float8_e4m3fn, 7), "e5m2": (ml_dtypes.float8_e5m2, 14)}[fmt]
    v = np.moveaxis(np.asarray(x, np.float32).astype(ml_dtypes.bfloat16).astype(np.float64), axis, -1)
    blocks = v.reshape(v.shape[:-1] + (-1, 32))
    amax = np.abs(blocks).max(-1, keepdims=True)
    byte = np.maximum(np.where(amax > 0, np.frexp(amax)[1] - 1 + 127, 0) - down, 1)
    scale = np.exp2(byte - 127.0)
    codes = (blocks / scale).astype(np.float32).astype(dtype).astype(np.float64)
    return np.moveaxis((codes * scale).reshape(v.shape), -1, axis)


WIDE = False


def mx_kscale(k):
    if not WIDE:
        return np.ones(k)
    levels = np.array([10, -10, 5, -5, 0])
    if k % 512:
        return np.exp2(np.random.permutation(np.resize(levels, k // 32))).repeat(32)
    a = np.empty((k // 512, 16))
    for p in range(k // 512):
        a[p, :8] = np.random.permutation(np.resize(levels, 8))
        for g in range(8):
            far = levels[np.abs(levels - a[p, g]) >= 10]
            a[p, g + 8] = far[np.random.randint(len(far))]
    return np.exp2(a.ravel()).repeat(32)


def f64(x):
    return np.asarray(x).astype(np.float64)


def striped8(idx):
    return np.asarray(idx).reshape(8, -1, 16).transpose(0, 2, 1).reshape(128, -1).astype(np.uint16)


def unstriped8(offs):
    return offs.reshape(8, 16, -1).transpose(0, 2, 1).reshape(8, -1).astype(np.int64)


def pick8(x, idx, run):
    r = np.arange(len(x))
    return x[r[:, None], idx[r % (8 * run) // run]]


E2M1 = np.array([0.0, 0.5, 1.0, 1.5, 2.0, 3.0, 4.0, 6.0, -0.0, -0.5, -1.0, -1.5, -2.0, -3.0, -4.0, -6.0])


def pack_weight(w, fmt):
    k, n = w.shape
    w = f64(np.asarray(w, np.float32).astype(ml_dtypes.bfloat16)).reshape(k // 32, 32, n)
    amax = np.abs(w).max(1)
    if fmt == "e4m3":
        byte = np.frexp(amax)[1] - 1 + 127 - 7
    else:
        mant, ex = np.frexp(amax / 6.0)
        byte = np.where(mant > 0.5, ex, ex - 1) + 127
    byte = np.clip(np.where(amax > 0, byte, 1), 1, 254)
    scaled = (w * np.exp2(127.0 - byte)[:, None, :]).reshape(k, n).astype(np.float32)
    by_word = np.ascontiguousarray(scaled.reshape(k // 512, 128, 4, n).transpose(0, 1, 3, 2))
    if fmt == "e4m3":
        words = by_word.astype(ml_dtypes.float8_e4m3fn).view(np.uint8)
    else:
        c = by_word.astype(ml_dtypes.float4_e2m1fn).view(np.uint8) & 0xF
        words = (c[..., 0::2] | (c[..., 1::2] << 4)).reshape(k // 512, 128, 2 * n)
    return np.ascontiguousarray(words), np.ascontiguousarray(byte.astype(np.uint8).reshape(k // 512, 16, n))


def unpack_weight(words, scales, fmt):
    g, _, n = scales.shape
    words = np.ascontiguousarray(words).reshape(g, 128, n, -1)
    if fmt == "e4m3":
        vals = words.view(ml_dtypes.float8_e4m3fn).astype(np.float64)
    else:
        nib = np.empty((g, 128, n, 4), np.uint8)
        nib[..., 0::2] = words & 0xF
        nib[..., 1::2] = words >> 4
        vals = E2M1[nib]
    vals = vals * np.repeat(np.exp2(scales.astype(np.float64) - 127.0), 8, axis=1)[..., None]
    return vals.transpose(0, 1, 3, 2).reshape(g * 512, n)


D, T, I, Q = 512, 1024, 512, 128


def setup_inputs():
    n = np.random.standard_normal
    idx = np.stack([np.random.permutation(T)[:I] for _ in range(8)])
    idx2 = np.stack([np.random.permutation(T)[:I] for _ in range(8)])
    idx3 = np.stack([np.random.permutation(T)[:I] for _ in range(8)])
    fd = mx_kscale(D)
    keysp = pack_weight(n((D, T)) / fd[:, None], "e2m1")
    return {
        "query": (n((D, Q)) * 0.9 / np.sqrt(D) * fd[:, None]).astype(np.float32),
        "query2": (n((D, Q)) * 0.9 / np.sqrt(D) * fd[:, None]).astype(np.float32),
        "keys_words": keysp[0],
        "keys_scales": keysp[1],
        "lam": (np.random.uniform(0.5, 1.5, (Q, 1))).astype(np.float32),
        "old": (1.0 * n((Q, T))).astype(np.float32),
        "offs": striped8(idx),
        "offs2": striped8(idx2),
        "offs3": striped8(idx3),
    }


def reference(query, query2, keys_words, keys_scales, lam, old, offs, offs2, offs3):
    idx = unstriped8(offs)
    idx2 = unstriped8(offs2)
    idx3 = unstriped8(offs3)
    keysu = unpack_weight(keys_words, keys_scales, "e2m1")
    queryq = mxq(f64(query), 0, "e4m3")
    a = queryq.T @ keysu
    query2q = mxq(f64(query2), 0, "e4m3")
    b = query2q.T @ keysu
    w = pick8(a, idx, 16) + pick8(a, idx2, 16) * np.tanh(pick8(b, idx, 16)) * f64(lam)
    f1 = np.zeros((Q, T))
    f1[np.arange(Q)[:, None], idx[np.arange(Q) % 128 // 16]] = w
    f2 = f1 + f64(old)
    y = pick8(f2, idx3, 16)
    return y

@@ -1,0 +1,142 @@
+from contextlib import ExitStack
+
+import concourse.mybir as mybir
+
+D, T, SLOTS, Q = 512, 1024, 512, 128
+FLOPS = 2 * 2 * D * Q * T
+
+F32 = mybir.dt.float32
+BF16 = mybir.dt.bfloat16
+I32 = mybir.dt.int32
+U32 = mybir.dt.uint32
+U16 = mybir.dt.uint16
+U8 = mybir.dt.uint8
+FP8X4 = mybir.dt.float8_e4m3fn_x4
+FP4X4 = mybir.dt.float4_e2m1fn_x4
+ACT = mybir.ActivationFunctionType
+ALU = mybir.AluOpType
+
+P = 128
+PACK = 4
+N_PASS = 256
+HALF = SLOTS // 2
+PER_COL = 16
+
+
+def tile_attend_turnedby_lean_through_heads_kernel(tc, query, query2, keys_words, keys_scales, lam, old, offs, offs2, offs3, out):
+    nc = tc.nc
+    with ExitStack() as ctx:
+        keep = ctx.enter_context(tc.tile_pool(name="keep", bufs=1))
+        psum = ctx.enter_context(tc.psum_pool(name="psum", bufs=1))
+
+        k_scales = keep.tile([P, T], U8, name="k_scales", align_bytes=64)
+        nc.vector.memset(k_scales[:].bitcast(I32), 0)
+
+        q2_raw = keep.tile([P, PACK, Q], F32, name="q2_raw")
+        nc.sync.dma_start(q2_raw[:], query2.rearrange("(p j) q -> p j q", j=PACK))
+        q_raw = keep.tile([P, PACK, Q], F32, name="q_raw")
+        nc.sync.dma_start(q_raw[:], query.rearrange("(p j) q -> p j q", j=PACK))
+        words32 = keys_words[0].bitcast(I32)
+        k_lo = keep.tile([P, T], U8, name="k_lo", align_bytes=64)
+        nc.sync.dma_start(k_lo[:].bitcast(I32), words32[:, 0 : T // 4])
+        scales32 = keys_scales[0].bitcast(I32)
+        for quad in range(4):
+            nc.sync.dma_start(k_scales[32 * quad : 32 * quad + 4, :].bitcast(I32), scales32[4 * quad : 4 * quad + 4, :])
+        k_hi = keep.tile([P, T], U8, name="k_hi", tag="late", align_bytes=64)
+        nc.sync.dma_start(k_hi[:].bitcast(I32), words32[:, T // 4 : T // 2])
+        k_words = [k_lo, k_hi]
+
+        warm_in = keep.tile([P, 1], F32, name="warm_in")
+        nc.gpsimd.memset(warm_in[:], 0.0)
+        warm_out = keep.tile([P, 1], F32, name="warm_out")
+        nc.scalar.activation(warm_out[:], warm_in[:], ACT.Sigmoid)
+
+        idx = keep.tile([P, SLOTS // PER_COL], U16, name="idx")
+        nc.sync.dma_start(idx[:], offs)
+        lam_col = keep.tile([P, 1], F32, name="lam_col")
+        nc.sync.dma_start(lam_col[:], lam)
+        idx2 = keep.tile([P, SLOTS // PER_COL], U16, name="idx2")
+        nc.sync.dma_start(idx2[:], offs2)
+        old_sb = keep.tile([P, T], F32, name="old_sb")
+        nc.sync.dma_start(old_sb[:], old)
+        idx3 = keep.tile([P, SLOTS // PER_COL], U16, name="idx3")
+        nc.sync.dma_start(idx3[:], offs3)
+
+        lam_twice = keep.tile([P, 1], F32, name="lam_twice")
+        nc.gpsimd.tensor_scalar(lam_twice[:], lam_col[:], 2.0, 0.0, ALU.mult, ALU.add)
+        lam_minus = keep.tile([P, 1], F32, name="lam_minus")
+        nc.gpsimd.tensor_scalar(lam_minus[:], lam_col[:], -1.0, 0.0, ALU.mult, ALU.add)
+
+        f1 = keep.tile([P, T], F32, name="f1")
+        nc.vector.memset(f1[:], 0.0)
+
+        q2_bf = keep.tile([P, Q, PACK], BF16, name="q2_bf", align_bytes=64)
+        nc.vector.tensor_copy(q2_bf[:], q2_raw[:].rearrange("p j q -> p q j"))
+        q2_codes = keep.tile([P, Q], U32, name="q2_codes", align_bytes=64)
+        q2_scales = keep.tile([P, Q], U8, name="q2_scales", align_bytes=64)
+        nc.vector.quantize_mx(q2_codes[:].bitcast(FP8X4), q2_scales[:], q2_bf[:].rearrange("p q j -> p (q j)"))
+
+        q_bf = keep.tile([P, Q, PACK], BF16, name="q_bf", align_bytes=64)
+        nc.scalar.copy(q_bf[:], q_raw[:].rearrange("p j q -> p q j"))
+        q_codes = keep.tile([P, Q], U32, name="q_codes", align_bytes=64)
+        q_scales = keep.tile([P, Q], U8, name="q_scales", align_bytes=64)
+        nc.vector.quantize_mx(q_codes[:].bitcast(FP8X4), q_scales[:], q_bf[:].rearrange("p q j -> p (q j)"))
+
+        def scores(codes, scales, table, pieces):
+            start = 0
+            for width, bank_id, engine in pieces:
+                cols = slice(start, start + width)
+                half, first = divmod(start, T // 2)
+                bank = psum.tile([P, width], F32, name=f"bank{bank_id}")
+                nc.tensor.matmul_mx(
+                    bank[:],
+                    lhsT=codes[:].bitcast(FP8X4),
+                    lhsT_scale=scales[:],
+                    rhs=k_words[half][:, 2 * first : 2 * (first + width)].bitcast(FP4X4),
+                    rhs_scale=k_scales[:, cols],
+                    start=True,
+                    stop=True,
+                )
+                engine(table[:, cols], bank[:])
+                start = start + width
+
+        b_sb = keep.tile([P, T], F32, name="b_sb")
+        a_sb = keep.tile([P, T], F32, name="a_sb")
+        on_v, on_s = nc.vector.tensor_copy, nc.scalar.copy
+        scores(q2_codes, q2_scales, b_sb, [(256, 0, on_v), (256, 1, on_s), (256, 2, on_v), (128, 3, on_s), (128, 4, on_v)])
+        scores(q_codes, q_scales, a_sb, [(256, 5, on_v), (256, 6, on_v), (256, 7, on_v), (128, 0, on_v), (128, 1, on_v)])
+
+        def lists(tile, h):
+            return tile[:, h * HALF // PER_COL : (h + 1) * HALF // PER_COL]
+
+        s0 = keep.tile([P, HALF], F32, name="s0")
+        nc.scalar.activation(s0[:], b_sb[:].indirect(lists(idx, 0)), ACT.Sigmoid, scale=2.0)
+        t0 = keep.tile([P, HALF], F32, name="t0", tag="late", align_bytes=64)
+        nc.vector.tensor_scalar(t0[:], s0[:], -0.5, lam_twice[:], ALU.add, ALU.mult)
+        u0 = keep.tile([P, HALF], F32, name="u0")
+        nc.vector.tensor_tensor(u0[:], a_sb[:].indirect(lists(idx2, 0)), t0[:], ALU.mult)
+        s1 = keep.tile([P, HALF], F32, name="s1")
+        nc.scalar.activation(s1[:], b_sb[:].indirect(lists(idx, 1)), ACT.Sigmoid, scale=2.0)
+        g0 = keep.tile([P, HALF], F32, name="g0")
+        nc.scalar.activation(g0[:], a_sb[:].indirect(lists(idx, 0)), ACT.Copy)
+        nc.vector.tensor_tensor(f1[:].indirect(lists(idx, 0)), g0[:], u0[:], ALU.add)
+
+        h1 = keep.tile([P, HALF], F32, name="h1")
+        nc.scalar.activation(h1[:], a_sb[:].indirect(lists(idx2, 1)), ACT.Copy)
+        t1 = keep.tile([P, HALF], F32, name="t1", tag="late", align_bytes=64)
+        nc.scalar.activation(t1[:], s1[:], ACT.Identity, scale=lam_twice[:], bias=lam_minus[:])
+        g1 = keep.tile([P, HALF], F32, name="g1")
+        nc.scalar.activation(g1[:], a_sb[:].indirect(lists(idx, 1)), ACT.Copy)
+        u1 = keep.tile([P, HALF], F32, name="u1")
+        nc.vector.tensor_tensor(u1[:], h1[:], t1[:], ALU.mult)
+        nc.vector.tensor_tensor(f1[:].indirect(lists(idx, 1)), g1[:], u1[:], ALU.add)
+
+        f2 = keep.tile([P, T], F32, name="f2")
+        nc.vector.tensor_tensor(f2[:], f1[:], old_sb[:], ALU.add)
+
+        y0 = keep.tile([P, HALF], F32, name="y0")
+        nc.vector.tensor_copy(y0[:], f2[:].indirect(lists(idx3, 0)))
+        nc.sync.dma_start(out[:, 0:HALF], y0[:])
+        y1 = keep.tile([P, HALF], F32, name="y1")
+        nc.scalar.activation(y1[:], f2[:].indirect(lists(idx3, 1)), ACT.Copy)
+        nc.scalar.dma_start(out[:, HALF:SLOTS], y1[:])

@@ -21,6 +21,8 @@ PACK = 4
 N_PASS = 256
 HALF = SLOTS // 2
 PER_COL = 16
+K_FIRST = 512
+Q_ON_VECTOR = 80
 
 
 def tile_attend_turnedby_lean_through_heads_kernel(tc, query, query2, keys_words, keys_scales, lam, old, offs, offs2, offs3, out):
@@ -34,17 +36,16 @@ def tile_attend_turnedby_lean_through_heads_kernel(tc, query, query2, keys_words
 
         q2_raw = keep.tile([P, PACK, Q], F32, name="q2_raw")
         nc.sync.dma_start(q2_raw[:], query2.rearrange("(p j) q -> p j q", j=PACK))
-        q_raw = keep.tile([P, PACK, Q], F32, name="q_raw")
-        nc.sync.dma_start(q_raw[:], query.rearrange("(p j) q -> p j q", j=PACK))
         words32 = keys_words[0].bitcast(I32)
-        k_lo = keep.tile([P, T], U8, name="k_lo", align_bytes=64)
-        nc.sync.dma_start(k_lo[:].bitcast(I32), words32[:, 0 : T // 4])
+        k_first = keep.tile([P, 2 * K_FIRST], U8, name="k_first", align_bytes=64)
+        nc.sync.dma_start(k_first[:].bitcast(I32), words32[:, 0 : K_FIRST // 2])
         scales32 = keys_scales[0].bitcast(I32)
         for quad in range(4):
             nc.sync.dma_start(k_scales[32 * quad : 32 * quad + 4, :].bitcast(I32), scales32[4 * quad : 4 * quad + 4, :])
-        k_hi = keep.tile([P, T], U8, name="k_hi", tag="late", align_bytes=64)
-        nc.sync.dma_start(k_hi[:].bitcast(I32), words32[:, T // 4 : T // 2])
-        k_words = [k_lo, k_hi]
+        q_raw = keep.tile([P, PACK, Q], F32, name="q_raw")
+        nc.sync.dma_start(q_raw[:], query.rearrange("(p j) q -> p j q", j=PACK))
+        k_rest = keep.tile([P, 2 * (T - K_FIRST)], U8, name="k_rest", tag="late", align_bytes=64)
+        nc.sync.dma_start(k_rest[:].bitcast(I32), words32[:, K_FIRST // 2 : T // 2])
 
         warm_in = keep.tile([P, 1], F32, name="warm_in")
         nc.gpsimd.memset(warm_in[:], 0.0)
@@ -64,35 +65,36 @@ def tile_attend_turnedby_lean_through_heads_kernel(tc, query, query2, keys_words
 
         lam_twice = keep.tile([P, 1], F32, name="lam_twice")
         nc.gpsimd.tensor_scalar(lam_twice[:], lam_col[:], 2.0, 0.0, ALU.mult, ALU.add)
-        lam_minus = keep.tile([P, 1], F32, name="lam_minus")
-        nc.gpsimd.tensor_scalar(lam_minus[:], lam_col[:], -1.0, 0.0, ALU.mult, ALU.add)
 
         f1 = keep.tile([P, T], F32, name="f1")
         nc.vector.memset(f1[:], 0.0)
 
-        q2_bf = keep.tile([P, Q, PACK], BF16, name="q2_bf", align_bytes=64)
-        nc.vector.tensor_copy(q2_bf[:], q2_raw[:].rearrange("p j q -> p q j"))
-        q2_codes = keep.tile([P, Q], U32, name="q2_codes", align_bytes=64)
-        q2_scales = keep.tile([P, Q], U8, name="q2_scales", align_bytes=64)
-        nc.vector.quantize_mx(q2_codes[:].bitcast(FP8X4), q2_scales[:], q2_bf[:].rearrange("p q j -> p (q j)"))
+        def quantise(name, raw, shares):
+            rounded = keep.tile([P, Q, PACK], BF16, name=f"{name}_bf", align_bytes=64)
+            for engine, cols in shares:
+                engine(
+                    rounded[:, cols, :].rearrange("p (c i) j -> p c j i", i=4),
+                    raw[:, :, cols].rearrange("p j (c i) -> p c j i", i=4),
+                )
+            codes = keep.tile([P, Q], U32, name=f"{name}_codes", align_bytes=64)
+            scales = keep.tile([P, Q], U8, name=f"{name}_scales", align_bytes=64)
+            nc.vector.quantize_mx(codes[:].bitcast(FP8X4), scales[:], rounded[:].rearrange("p q j -> p (q j)"))
+            return codes, scales
 
-        q_bf = keep.tile([P, Q, PACK], BF16, name="q_bf", align_bytes=64)
-        nc.scalar.copy(q_bf[:], q_raw[:].rearrange("p j q -> p q j"))
-        q_codes = keep.tile([P, Q], U32, name="q_codes", align_bytes=64)
-        q_scales = keep.tile([P, Q], U8, name="q_scales", align_bytes=64)
-        nc.vector.quantize_mx(q_codes[:].bitcast(FP8X4), q_scales[:], q_bf[:].rearrange("p q j -> p (q j)"))
+        q2_codes, q2_scales = quantise("q2", q2_raw, [(nc.vector.tensor_copy, slice(0, Q_ON_VECTOR)), (nc.scalar.copy, slice(Q_ON_VECTOR, Q))])
+        q_codes, q_scales = quantise("q", q_raw, [(nc.vector.tensor_copy, slice(0, Q))])
 
         def scores(codes, scales, table, pieces):
             start = 0
             for width, bank_id, engine in pieces:
                 cols = slice(start, start + width)
-                half, first = divmod(start, T // 2)
+                words, first = (k_first, start) if start < K_FIRST else (k_rest, start - K_FIRST)
                 bank = psum.tile([P, width], F32, name=f"bank{bank_id}")
                 nc.tensor.matmul_mx(
                     bank[:],
                     lhsT=codes[:].bitcast(FP8X4),
                     lhsT_scale=scales[:],
-                    rhs=k_words[half][:, 2 * first : 2 * (first + width)].bitcast(FP4X4),
+                    rhs=words[:, 2 * first : 2 * (first + width)].bitcast(FP4X4),
                     rhs_scale=k_scales[:, cols],
                     start=True,
                     stop=True,
@@ -103,13 +105,13 @@ def tile_attend_turnedby_lean_through_heads_kernel(tc, query, query2, keys_words
         b_sb = keep.tile([P, T], F32, name="b_sb")
         a_sb = keep.tile([P, T], F32, name="a_sb")
         on_v, on_s = nc.vector.tensor_copy, nc.scalar.copy
-        scores(q2_codes, q2_scales, b_sb, [(256, 0, on_v), (256, 1, on_s), (256, 2, on_v), (128, 3, on_s), (128, 4, on_v)])
+        scores(q2_codes, q2_scales, b_sb, [(256, 0, on_s), (256, 1, on_s), (256, 2, on_s), (128, 3, on_v), (128, 4, on_v)])
         scores(q_codes, q_scales, a_sb, [(256, 5, on_v), (256, 6, on_v), (256, 7, on_v), (128, 0, on_v), (128, 1, on_v)])
 
         def lists(tile, h):
             return tile[:, h * HALF // PER_COL : (h + 1) * HALF // PER_COL]
 
-        s0 = keep.tile([P, HALF], F32, name="s0")
+        s0 = keep.tile([P, HALF], F32, name="s0", tag="first_s")
         nc.scalar.activation(s0[:], b_sb[:].indirect(lists(idx, 0)), ACT.Sigmoid, scale=2.0)
         t0 = keep.tile([P, HALF], F32, name="t0", tag="late", align_bytes=64)
         nc.vector.tensor_scalar(t0[:], s0[:], -0.5, lam_twice[:], ALU.add, ALU.mult)
@@ -117,14 +119,14 @@ def tile_attend_turnedby_lean_through_heads_kernel(tc, query, query2, keys_words
         nc.vector.tensor_tensor(u0[:], a_sb[:].indirect(lists(idx2, 0)), t0[:], ALU.mult)
         s1 = keep.tile([P, HALF], F32, name="s1")
         nc.scalar.activation(s1[:], b_sb[:].indirect(lists(idx, 1)), ACT.Sigmoid, scale=2.0)
+        t1 = keep.tile([P, HALF], F32, name="t1", tag="first_s")
+        nc.vector.tensor_scalar(t1[:], s1[:], -0.5, lam_twice[:], ALU.add, ALU.mult)
         g0 = keep.tile([P, HALF], F32, name="g0")
         nc.scalar.activation(g0[:], a_sb[:].indirect(lists(idx, 0)), ACT.Copy)
         nc.vector.tensor_tensor(f1[:].indirect(lists(idx, 0)), g0[:], u0[:], ALU.add)
 
         h1 = keep.tile([P, HALF], F32, name="h1")
         nc.scalar.activation(h1[:], a_sb[:].indirect(lists(idx2, 1)), ACT.Copy)
-        t1 = keep.tile([P, HALF], F32, name="t1", tag="late", align_bytes=64)
-        nc.scalar.activation(t1[:], s1[:], ACT.Identity, scale=lam_twice[:], bias=lam_minus[:])
         g1 = keep.tile([P, HALF], F32, name="g1")
         nc.scalar.activation(g1[:], a_sb[:].indirect(lists(idx, 1)), ACT.Copy)
         u1 = keep.tile([P, HALF], F32, name="u1")

from contextlib import ExitStack

import concourse.mybir as mybir

D, T, SLOTS, Q = 512, 1024, 512, 128
FLOPS = 2 * 2 * D * Q * T

F32 = mybir.dt.float32
BF16 = mybir.dt.bfloat16
I32 = mybir.dt.int32
U32 = mybir.dt.uint32
U16 = mybir.dt.uint16
U8 = mybir.dt.uint8
FP8X4 = mybir.dt.float8_e4m3fn_x4
FP4X4 = mybir.dt.float4_e2m1fn_x4
ACT = mybir.ActivationFunctionType
ALU = mybir.AluOpType

P = 128
PACK = 4
N_PASS = 256
HALF = SLOTS // 2
PER_COL = 16
K_FIRST = 512
Q_ON_VECTOR = 80


def tile_attend_turnedby_lean_through_heads_kernel(tc, query, query2, keys_words, keys_scales, lam, old, offs, offs2, offs3, out):
    nc = tc.nc
    with ExitStack() as ctx:
        keep = ctx.enter_context(tc.tile_pool(name="keep", bufs=1))
        psum = ctx.enter_context(tc.psum_pool(name="psum", bufs=1))

        k_scales = keep.tile([P, T], U8, name="k_scales", align_bytes=64)
        nc.vector.memset(k_scales[:].bitcast(I32), 0)

        q2_raw = keep.tile([P, PACK, Q], F32, name="q2_raw")
        nc.sync.dma_start(q2_raw[:], query2.rearrange("(p j) q -> p j q", j=PACK))
        words32 = keys_words[0].bitcast(I32)
        k_first = keep.tile([P, 2 * K_FIRST], U8, name="k_first", align_bytes=64)
        nc.sync.dma_start(k_first[:].bitcast(I32), words32[:, 0 : K_FIRST // 2])
        scales32 = keys_scales[0].bitcast(I32)
        for quad in range(4):
            nc.sync.dma_start(k_scales[32 * quad : 32 * quad + 4, :].bitcast(I32), scales32[4 * quad : 4 * quad + 4, :])
        q_raw = keep.tile([P, PACK, Q], F32, name="q_raw")
        nc.sync.dma_start(q_raw[:], query.rearrange("(p j) q -> p j q", j=PACK))
        k_rest = keep.tile([P, 2 * (T - K_FIRST)], U8, name="k_rest", tag="late", align_bytes=64)
        nc.sync.dma_start(k_rest[:].bitcast(I32), words32[:, K_FIRST // 2 : T // 2])

        warm_in = keep.tile([P, 1], F32, name="warm_in")
        nc.gpsimd.memset(warm_in[:], 0.0)
        warm_out = keep.tile([P, 1], F32, name="warm_out")
        nc.scalar.activation(warm_out[:], warm_in[:], ACT.Sigmoid)

        idx = keep.tile([P, SLOTS // PER_COL], U16, name="idx")
        nc.sync.dma_start(idx[:], offs)
        lam_col = keep.tile([P, 1], F32, name="lam_col")
        nc.sync.dma_start(lam_col[:], lam)
        idx2 = keep.tile([P, SLOTS // PER_COL], U16, name="idx2")
        nc.sync.dma_start(idx2[:], offs2)
        old_sb = keep.tile([P, T], F32, name="old_sb")
        nc.sync.dma_start(old_sb[:], old)
        idx3 = keep.tile([P, SLOTS // PER_COL], U16, name="idx3")
        nc.sync.dma_start(idx3[:], offs3)

        lam_twice = keep.tile([P, 1], F32, name="lam_twice")
        nc.gpsimd.tensor_scalar(lam_twice[:], lam_col[:], 2.0, 0.0, ALU.mult, ALU.add)

        f1 = keep.tile([P, T], F32, name="f1")
        nc.vector.memset(f1[:], 0.0)

        def quantise(name, raw, shares):
            rounded = keep.tile([P, Q, PACK], BF16, name=f"{name}_bf", align_bytes=64)
            for engine, cols in shares:
                engine(
                    rounded[:, cols, :].rearrange("p (c i) j -> p c j i", i=4),
                    raw[:, :, cols].rearrange("p j (c i) -> p c j i", i=4),
                )
            codes = keep.tile([P, Q], U32, name=f"{name}_codes", align_bytes=64)
            scales = keep.tile([P, Q], U8, name=f"{name}_scales", align_bytes=64)
            nc.vector.quantize_mx(codes[:].bitcast(FP8X4), scales[:], rounded[:].rearrange("p q j -> p (q j)"))
            return codes, scales

        q2_codes, q2_scales = quantise("q2", q2_raw, [(nc.vector.tensor_copy, slice(0, Q_ON_VECTOR)), (nc.scalar.copy, slice(Q_ON_VECTOR, Q))])
        q_codes, q_scales = quantise("q", q_raw, [(nc.vector.tensor_copy, slice(0, Q))])

        def scores(codes, scales, table, pieces):
            start = 0
            for width, bank_id, engine in pieces:
                cols = slice(start, start + width)
                words, first = (k_first, start) if start < K_FIRST else (k_rest, start - K_FIRST)
                bank = psum.tile([P, width], F32, name=f"bank{bank_id}")
                nc.tensor.matmul_mx(
                    bank[:],
                    lhsT=codes[:].bitcast(FP8X4),
                    lhsT_scale=scales[:],
                    rhs=words[:, 2 * first : 2 * (first + width)].bitcast(FP4X4),
                    rhs_scale=k_scales[:, cols],
                    start=True,
                    stop=True,
                )
                engine(table[:, cols], bank[:])
                start = start + width

        b_sb = keep.tile([P, T], F32, name="b_sb")
        a_sb = keep.tile([P, T], F32, name="a_sb")
        on_v, on_s = nc.vector.tensor_copy, nc.scalar.copy
        scores(q2_codes, q2_scales, b_sb, [(256, 0, on_s), (256, 1, on_s), (256, 2, on_s), (128, 3, on_v), (128, 4, on_v)])
        scores(q_codes, q_scales, a_sb, [(256, 5, on_v), (256, 6, on_v), (256, 7, on_v), (128, 0, on_v), (128, 1, on_v)])

        def lists(tile, h):
            return tile[:, h * HALF // PER_COL : (h + 1) * HALF // PER_COL]

        s0 = keep.tile([P, HALF], F32, name="s0", tag="first_s")
        nc.scalar.activation(s0[:], b_sb[:].indirect(lists(idx, 0)), ACT.Sigmoid, scale=2.0)
        t0 = keep.tile([P, HALF], F32, name="t0", tag="late", align_bytes=64)
        nc.vector.tensor_scalar(t0[:], s0[:], -0.5, lam_twice[:], ALU.add, ALU.mult)
        u0 = keep.tile([P, HALF], F32, name="u0")
        nc.vector.tensor_tensor(u0[:], a_sb[:].indirect(lists(idx2, 0)), t0[:], ALU.mult)
        s1 = keep.tile([P, HALF], F32, name="s1")
        nc.scalar.activation(s1[:], b_sb[:].indirect(lists(idx, 1)), ACT.Sigmoid, scale=2.0)
        t1 = keep.tile([P, HALF], F32, name="t1", tag="first_s")
        nc.vector.tensor_scalar(t1[:], s1[:], -0.5, lam_twice[:], ALU.add, ALU.mult)
        g0 = keep.tile([P, HALF], F32, name="g0")
        nc.scalar.activation(g0[:], a_sb[:].indirect(lists(idx, 0)), ACT.Copy)
        nc.vector.tensor_tensor(f1[:].indirect(lists(idx, 0)), g0[:], u0[:], ALU.add)

        h1 = keep.tile([P, HALF], F32, name="h1")
        nc.scalar.activation(h1[:], a_sb[:].indirect(lists(idx2, 1)), ACT.Copy)
        g1 = keep.tile([P, HALF], F32, name="g1")
        nc.scalar.activation(g1[:], a_sb[:].indirect(lists(idx, 1)), ACT.Copy)
        u1 = keep.tile([P, HALF], F32, name="u1")
        nc.vector.tensor_tensor(u1[:], h1[:], t1[:], ALU.mult)
        nc.vector.tensor_tensor(f1[:].indirect(lists(idx, 1)), g1[:], u1[:], ALU.add)

        f2 = keep.tile([P, T], F32, name="f2")
        nc.vector.tensor_tensor(f2[:], f1[:], old_sb[:], ALU.add)

        y0 = keep.tile([P, HALF], F32, name="y0")
        nc.vector.tensor_copy(y0[:], f2[:].indirect(lists(idx3, 0)))
        nc.sync.dma_start(out[:, 0:HALF], y0[:])
        y1 = keep.tile([P, HALF], F32, name="y1")
        nc.scalar.activation(y1[:], f2[:].indirect(lists(idx3, 1)), ACT.Copy)
        nc.scalar.dma_start(out[:, HALF:SLOTS], y1[:])
